import numpy as np
import ml_dtypes


def mxq(x, axis, fmt="e4m3"):
    dtype, down = {"e4m3": (ml_dtypes.float8_e4m3fn, 7), "e5m2": (ml_dtypes.float8_e5m2, 14)}[fmt]
    v = np.moveaxis(np.asarray(x, np.float32).astype(ml_dtypes.bfloat16).astype(np.float64), axis, -1)
    blocks = v.reshape(v.shape[:-1] + (-1, 32))
    amax = np.abs(blocks).max(-1, keepdims=True)
    byte = np.maximum(np.where(amax > 0, np.frexp(amax)[1] - 1 + 127, 0) - down, 1)
    scale = np.exp2(byte - 127.0)
    codes = (blocks / scale).astype(np.float32).astype(dtype).astype(np.float64)
    return np.moveaxis((codes * scale).reshape(v.shape), -1, axis)


WIDE = False


def mx_kscale(k):
    if not WIDE:
        return np.ones(k)
    levels = np.array([10, -10, 5, -5, 0])
    if k % 512:
        return np.exp2(np.random.permutation(np.resize(levels, k // 32))).repeat(32)
    a = np.empty((k // 512, 16))
    for p in range(k // 512):
        a[p, :8] = np.random.permutation(np.resize(levels, 8))
        for g in range(8):
            far = levels[np.abs(levels - a[p, g]) >= 10]
            a[p, g + 8] = far[np.random.randint(len(far))]
    return np.exp2(a.ravel()).repeat(32)


def f64(x):
    return np.asarray(x).astype(np.float64)


def striped(idx):
    return np.tile(idx.reshape(-1, 16).T, (8, 1)).astype(np.uint16)


def unstriped(offs):
    return offs[:16].T.reshape(-1).astype(np.int64)


E2M1 = np.array([0.0, 0.5, 1.0, 1.5, 2.0, 3.0, 4.0, 6.0, -0.0, -0.5, -1.0, -1.5, -2.0, -3.0, -4.0, -6.0])


def pack_weight(w, fmt):
    k, n = w.shape
    w = f64(np.asarray(w, np.float32).astype(ml_dtypes.bfloat16)).reshape(k // 32, 32, n)
    amax = np.abs(w).max(1)
    if fmt == "e4m3":
        byte = np.frexp(amax)[1] - 1 + 127 - 7
    else:
        mant, ex = np.frexp(amax / 6.0)
        byte = np.where(mant > 0.5, ex, ex - 1) + 127
    byte = np.clip(np.where(amax > 0, byte, 1), 1, 254)
    scaled = (w * np.exp2(127.0 - byte)[:, None, :]).reshape(k, n).astype(np.float32)
    by_word = np.ascontiguousarray(scaled.reshape(k // 512, 128, 4, n).transpose(0, 1, 3, 2))
    if fmt == "e4m3":
        words = by_word.astype(ml_dtypes.float8_e4m3fn).view(np.uint8)
    else:
        c = by_word.astype(ml_dtypes.float4_e2m1fn).view(np.uint8) & 0xF
        words = (c[..., 0::2] | (c[..., 1::2] << 4)).reshape(k // 512, 128, 2 * n)
    return np.ascontiguousarray(words), np.ascontiguousarray(byte.astype(np.uint8).reshape(k // 512, 16, n))


def unpack_weight(words, scales, fmt):
    g, _, n = scales.shape
    words = np.ascontiguousarray(words).reshape(g, 128, n, -1)
    if fmt == "e4m3":
        vals = words.view(ml_dtypes.float8_e4m3fn).astype(np.float64)
    else:
        nib = np.empty((g, 128, n, 4), np.uint8)
        nib[..., 0::2] = words & 0xF
        nib[..., 1::2] = words >> 4
        vals = E2M1[nib]
    vals = vals * np.repeat(np.exp2(scales.astype(np.float64) - 127.0), 8, axis=1)[..., None]
    return vals.transpose(0, 1, 3, 2).reshape(g * 512, n)


def gelu(v):
    return 0.5 * v * (1.0 + np.tanh(np.sqrt(2.0 / np.pi) * (v + 0.044715 * v**3)))


def striped8(idx):
    return np.concatenate([v.reshape(-1, 16).T for v in idx]).astype(np.uint16)


def unstriped8(offs):
    return np.stack([offs[16 * g:16 * g + 16].T.reshape(-1) for g in range(8)]).astype(np.int64)


def runs(v, idx8):
    k = np.arange(v.shape[0])
    return v[k[:, None], idx8[k % 512 // 64]]


K, M, H, T, S, T2 = 1024, 512, 1024, 2048, 1024, 2048


def setup_inputs():
    n = np.random.standard_normal
    s = mx_kscale(K)[:, None]
    s2 = mx_kscale(M)[:, None]
    u = mx_kscale(H)[:, None]
    tab_words, tab_scales = pack_weight(n((K, T)) * s, "e4m3")
    tab2_words, tab2_scales = pack_weight(n((M, T)) * s2, "e4m3")
    w2_words, w2_scales = pack_weight(1.2 * n((M, H)) / s2 / np.sqrt(M), "e2m1")
    w3_words, w3_scales = pack_weight(n((H, H)) / u / np.sqrt(H), "e4m3")
    return {
        "tab_words": tab_words, "tab_scales": tab_scales,
        "tab2_words": tab2_words, "tab2_scales": tab2_scales,
        "offs": striped8(np.stack([np.random.permutation(T)[:S] for _ in range(8)])),
        "offs2": striped(np.random.permutation(T)[:S]),
        "offs3": striped(np.random.permutation(T2)[:S]),
        "w1": (1.2 * n((K, H)) / s / np.sqrt(K)).astype(np.float32),
        "w2_words": w2_words, "w2_scales": w2_scales,
        "w3_words": w3_words, "w3_scales": w3_scales,
        "gain": (np.exp(0.4 * n(H)) * u[:, 0]).astype(np.float32),
        "page1": n((H, T2)).astype(np.float32),
        "wgo": np.exp(0.3 * n((128, S))).astype(np.float32),
    }


def reference(tab_words, tab_scales, tab2_words, tab2_scales, offs, offs2, offs3, w1, w2_words, w2_scales, w3_words, w3_scales, gain, page1, wgo):
    v = runs(unpack_weight(tab_words, tab_scales, "e4m3"), unstriped8(offs))
    v2 = unpack_weight(tab2_words, tab2_scales, "e4m3")[:, unstriped(offs2)]
    w2 = unpack_weight(w2_words, w2_scales, "e2m1")
    w3 = unpack_weight(w3_words, w3_scales, "e4m3")
    a = mxq(f64(w1), 0, "e4m3").T @ v
    b = w2.T @ v2
    e = np.exp(-np.abs(a - b))
    z = e * f64(gain)[:, None]
    y = (w3.T @ mxq(z, 0, "e4m3")) + e
    out = f64(page1).copy()
    out[:, unstriped(offs3)] = np.tile(f64(wgo), (H // 128, 1)) * y
    return out

@@ -1,0 +1,309 @@
+from contextlib import ExitStack
+
+import concourse.mybir as mybir
+
+K, M, H, T, S, T2 = 1024, 512, 1024, 2048, 1024, 2048
+FLOPS = 2 * S * H * (K + M + H)
+
+F32 = mybir.dt.float32
+BF16 = mybir.dt.bfloat16
+I32 = mybir.dt.int32
+U32 = mybir.dt.uint32
+U16 = mybir.dt.uint16
+U8 = mybir.dt.uint8
+FP8X4 = mybir.dt.float8_e4m3fn_x4
+FP4X4 = mybir.dt.float4_e2m1fn_x4
+ACT = mybir.ActivationFunctionType
+ALU = mybir.AluOpType
+
+P = 128
+PACK = 4
+PASS = P * PACK
+BANK = 512
+LANES = 16
+CHUNKS = ((0, 256), (256, 512), (512, 1024))
+GATHERS = ((0, 512), (512, 1024))
+
+
+def tile_list_retake_closeness_sheet_kernel(
+    tc, tab_words, tab_scales, tab2_words, tab2_scales, offs, offs2, offs3, w1,
+    w2_words, w2_scales, w3_words, w3_scales, gain, page1, wgo, out,
+):
+    nc = tc.nc
+    with ExitStack() as ctx:
+        lists = ctx.enter_context(tc.tile_pool(name="lists", bufs=1))
+        keep = ctx.enter_context(tc.tile_pool(name="keep", bufs=1))
+        stage = ctx.enter_context(tc.tile_pool(name="stage", bufs=11))
+        ring = ctx.enter_context(tc.tile_pool(name="ring", bufs=2))
+        psum = ctx.enter_context(tc.psum_pool(name="psum", bufs=4))
+
+        def big(shape, dtype, name):
+            return stage.tile(shape, dtype, name=name, tag="big", align_bytes=64)
+
+        def kept(shape, dtype, name):
+            return keep.tile(shape, dtype, name=name, align_bytes=64)
+
+        list1 = lists.tile([P, S // LANES], U16, name="list1")
+        list2 = lists.tile([P, S // LANES], U16, name="list2")
+        list3 = lists.tile([P, S // LANES], U16, name="list3")
+
+        def entries(list_tile, j0, j1):
+            return list_tile[:, j0 // LANES : j1 // LANES]
+
+        v_bytes = kept([P, T], U8, "v_bytes")
+        v2_bytes = kept([P, T], U8, "v2_bytes")
+        w2_bytes = kept([P, H], U8, "w2_bytes")
+        w3_bytes = kept([P, H], U8, "w3_bytes")
+        nc.vector.memset(v_bytes[:].bitcast(I32), 0)
+        nc.gpsimd.memset(v2_bytes[:].bitcast(I32), 0)
+        nc.vector.memset(w2_bytes[:].bitcast(I32), 0)
+        nc.vector.memset(w3_bytes[:].bitcast(I32), 0)
+        for a in range(2):
+            for r in range(2):
+                rows = tab_scales[a].rearrange("(g r) t -> r g t", r=2)[r]
+                nc.scalar.dma_start(v_bytes[:].bitcast(I32)[4 * a + r : P : LANES, :], rows.bitcast(I32))
+        for q in range(4):
+            nc.gpsimd.dma_start(
+                v2_bytes[:].bitcast(I32)[32 * q : 32 * q + 4, :], tab2_scales[0, 4 * q : 4 * q + 4, :].bitcast(I32)
+            )
+
+        def load_table(words, name):
+            table = big([P, T], I32, name)
+            nc.sync.dma_start(table[:], words.rearrange("p t i -> p (t i)").bitcast(I32))
+            return table
+
+        def load_w1(b, a):
+            raw = big([P, PACK, PASS], F32, "w1_raw%d%d" % (b, a))
+            rows = w1[PASS * a : PASS * (a + 1), PASS * b : PASS * (b + 1)]
+            nc.sync.dma_start(raw[:], rows.rearrange("(p i) c -> p i c", i=PACK))
+            return raw
+
+        def sheet_rows(sheet, b, t):
+            return sheet[PASS * b : PASS * (b + 1), :].rearrange("(p t) c -> p t c", t=PACK)[:, t, :]
+
+        def load_page(b, t):
+            page = big([P, T2], F32, "page%d%d" % (b, t))
+            nc.sync.dma_start(page[:], sheet_rows(page1, b, t))
+            return page
+
+        def load_wgo(j0, j1):
+            dealt = kept([P, PACK, j1 - j0], F32, "wgo%d" % j0)
+            for q in range(4):
+                nc.sync.dma_start(
+                    dealt[32 * q : 32 * (q + 1), :, :], wgo.rearrange("(i t) j -> i t j", t=PACK)[:, :, j0:j1]
+                )
+            return dealt
+
+        w1_raw = {}
+        nc.sync.dma_start(list1[:], offs)
+        nc.sync.dma_start(list2[:], offs2)
+        nc.sync.dma_start(list3[:], offs3)
+        gains = kept([P, 2, PACK], F32, "gains")
+        nc.sync.dma_start(gains[:], gain.rearrange("(b p t) -> p b t", b=2, t=PACK))
+        tables = [load_table(tab_words[0], "table0")]
+        w1_raw[0, 0] = load_w1(0, 0)
+        w2_raw = kept([P, 2 * H], U8, "w2_raw")
+        nc.sync.dma_start(w2_raw[:].bitcast(I32), w2_words[0].bitcast(I32))
+        tables.append(load_table(tab_words[1], "table1"))
+        w1_raw[0, 1] = load_w1(0, 1)
+        tables.append(load_table(tab2_words[0], "table2"))
+        for q in range(4):
+            nc.sync.dma_start(
+                w2_bytes[:].bitcast(I32)[32 * q : 32 * q + 4, :], w2_scales[0, 4 * q : 4 * q + 4, :].bitcast(I32)
+            )
+        w1_raw[1, 0] = load_w1(1, 0)
+        w1_raw[1, 1] = load_w1(1, 1)
+        for q in range(4):
+            nc.sync.dma_start(
+                w3_bytes[:].bitcast(I32)[32 * q : 32 * q + 8, :], w3_scales[:, 4 * q : 4 * q + 4, :].bitcast(I32)
+            )
+        w3_raw = big([P, 2, H], I32, "w3_raw")
+        nc.sync.dma_start(w3_raw[:], w3_words.rearrange("a p c i -> p a (c i)").bitcast(I32))
+        first = CHUNKS[0][1]
+        wgo_first = load_wgo(0, first)
+        order = [(b, t) for t in range(PACK) for b in range(2)]
+        pages = {}
+        for b, t in order[:4]:
+            pages[b, t] = load_page(b, t)
+        wgo_rest = load_wgo(first, S)
+        for b, t in order[4:]:
+            pages[b, t] = load_page(b, t)
+
+        def wgo_cols(t, j0, j1):
+            if j1 <= first:
+                return wgo_first[:, t, j0:j1]
+            return wgo_rest[:, t, j0 - first : j1 - first]
+
+        v_picked = kept([P, S], U8, "v_picked")
+        nc.vector.tensor_copy(v_picked[:], v_bytes[:].indirect(list1[:]))
+        v_planes = kept([P, S], U8, "v_planes")
+        nc.vector.tensor_copy(v_planes[:].bitcast(I32), v_picked[:].bitcast(I32))
+        for a in range(2):
+            for r in range(2):
+                nc.gpsimd.dma_start(
+                    v_planes[:].bitcast(I32)[4 * a + 2 + r : P : 32, :],
+                    v_picked[:].bitcast(I32)[LANES + 4 * a + r : P : 32, :],
+                )
+        v2_plane = kept([P, S], U8, "v2_plane")
+        nc.vector.tensor_copy(v2_plane[:], v2_bytes[:].indirect(list2[:]))
+
+        picked = {}
+
+        def gather_words(part):
+            j0, j1 = GATHERS[part]
+            for n, (table, list_tile) in enumerate(zip(tables, (list1, list1, list2))):
+                words = kept([P, j1 - j0], I32, "picked%d%d" % (n, part))
+                nc.vector.tensor_copy(
+                    words[:].bitcast(U32), table[:].bitcast(U32).indirect(entries(list_tile, j0, j1))
+                )
+                picked[n, part] = words
+
+        def picked_cols(n, j0, j1):
+            part = 0 if j1 <= GATHERS[0][1] else 1
+            base = GATHERS[part][0]
+            return picked[n, part][:, j0 - base : j1 - base].bitcast(FP8X4)
+
+        gather_words(0)
+
+        def deal_bytes(raw, name):
+            dealt = kept([P, H], U8, name)
+            nc.vector.tensor_copy(
+                dealt[:].rearrange("p (b t m) -> p b m t", b=2, t=PACK),
+                raw[:].rearrange("p (b m t) -> p b m t", b=2, t=PACK),
+            )
+            return dealt
+
+        w2_plane = deal_bytes(w2_bytes, "w2_plane")
+        w2_codes = kept([P, 2 * H], U8, "w2_codes")
+        nc.vector.tensor_copy(
+            w2_codes[:].rearrange("p (b t m e) -> p b m t e", b=2, t=PACK, e=2),
+            w2_raw[:].rearrange("p (b m t e) -> p b m t e", b=2, t=PACK, e=2),
+        )
+
+        w1_codes, w1_plane = {}, {}
+        for b in range(2):
+            for a in range(2):
+                rounded = ring.tile([P, PACK * PASS], BF16, name="w1_rounded", align_bytes=64)
+                dst = rounded[:].rearrange("p (t m i) -> p m t i", t=PACK, i=PACK)
+                src = w1_raw[b, a][:].rearrange("p i (m t) -> p m t i", t=PACK)
+                if (b, a) == (1, 1):
+                    nc.vector.tensor_scalar_mul(dst, src, -1.0)
+                else:
+                    nc.scalar.activation(dst, src, ACT.Copy, scale=-1.0)
+                w1_codes[b, a] = kept([P, PASS], U32, "w1_codes%d%d" % (b, a))
+                w1_plane[b, a] = kept([P, PASS], U8, "w1_plane%d%d" % (b, a))
+                nc.vector.quantize_mx(w1_codes[b, a][:].bitcast(FP8X4), w1_plane[b, a][:], rounded[:])
+
+        w3_planes = deal_bytes(w3_bytes, "w3_planes")
+        w3_codes = kept([P, 2 * H], I32, "w3_codes")
+        nc.vector.tensor_copy(
+            w3_codes[:].bitcast(U32).rearrange("p (h t m) -> p h m t", t=PACK, m=P),
+            w3_raw[:].bitcast(U32).rearrange("p a (b m t) -> p (a b) m t", t=PACK, m=P),
+        )
+
+        def first_stage(c):
+            j0, j1 = CHUNKS[c]
+            width = j1 - j0
+            per_bank = BANK // width
+            close = kept([P, 2, PACK, width], F32, "close%d" % c)
+            z_ops = []
+            for b in range(2):
+                for t0 in range(0, PACK, per_bank):
+                    bank = psum.tile([P, BANK], F32, name="diff")
+                    for s in range(per_bank):
+                        t = t0 + s
+                        acc = bank[:, s * width : (s + 1) * width]
+                        col = PASS * b + P * t
+                        nc.tensor.matmul_mx(
+                            acc, lhsT=w2_codes[:, 2 * col : 2 * (col + P)].bitcast(FP4X4),
+                            lhsT_scale=w2_plane[:, col : col + P],
+                            rhs=picked_cols(2, j0, j1), rhs_scale=v2_plane[:, j0:j1], start=True, stop=False,
+                        )
+                        for a in range(2):
+                            nc.tensor.matmul_mx(
+                                acc, lhsT=w1_codes[b, a][:, P * t : P * (t + 1)].bitcast(FP8X4),
+                                lhsT_scale=w1_plane[b, a][:, P * t : P * (t + 1)],
+                                rhs=picked_cols(a, j0, j1), rhs_scale=v_planes[4 * a : P, j0:j1],
+                                start=False, stop=(a == 1),
+                            )
+                    part = close[:, b, t0 : t0 + per_bank, :].rearrange("p t j -> p (t j)")
+                    nc.scalar.activation(part, bank[:], ACT.Abs)
+                    nc.scalar.activation(part, part, ACT.Exp, scale=-1.0)
+                if c > 0 and b == 1:
+                    woven = keep.tile([P, PACK * width], BF16, name="woven_last", tag="turn%d" % c, align_bytes=64)
+                else:
+                    woven = ring.tile([P, PACK * width], BF16, name="woven", align_bytes=64)
+                walk_out = woven[:].rearrange("p (c i t) -> p c t i", t=PACK, i=4)
+                if c == 0:
+                    nc.vector.tensor_tensor(
+                        walk_out,
+                        close[:, b].rearrange("p t (c i) -> p c t i", i=4),
+                        gains[:, b, :].unsqueeze(1).unsqueeze(3).to_broadcast([P, width // 4, PACK, 4]),
+                        ALU.mult,
+                    )
+                else:
+                    scaled = ring.tile([P, PACK, width], BF16, name="scaled", align_bytes=64)
+                    for t in range(PACK):
+                        nc.scalar.activation(
+                            scaled[:, t, :], close[:, b, t, :], ACT.Copy, scale=gains[:, b, t : t + 1]
+                        )
+                    nc.scalar.copy(walk_out, scaled[:].rearrange("p t (c i) -> p c t i", i=4))
+                z_codes = kept([P, width], U32, "z_codes%d%d" % (c, b))
+                z_plane = kept([P, width], U8, "z_plane%d%d" % (c, b))
+                nc.vector.quantize_mx(z_codes[:].bitcast(FP8X4), z_plane[:], woven[:])
+                z_ops.append((z_codes, z_plane))
+            return close, z_ops
+
+        def add_residual(c, close, z_ops, unit):
+            j0, j1 = CHUNKS[c]
+            width = j1 - j0
+            per_bank = BANK // width
+            t, b0 = divmod(unit * per_bank, 2)
+            bank = psum.tile([P, BANK], F32, name="mixed")
+            for s in range(per_bank):
+                col = PASS * (b0 + s) + P * t
+                for a in range(2):
+                    nc.tensor.matmul_mx(
+                        bank[:, s * width : (s + 1) * width],
+                        lhsT=w3_codes[:, H * a + col : H * a + col + P].bitcast(FP8X4),
+                        lhsT_scale=w3_planes[4 * a : P, col : col + P],
+                        rhs=z_ops[a][0][:].bitcast(FP8X4), rhs_scale=z_ops[a][1][:],
+                        start=(a == 0), stop=(a == 1),
+                    )
+            if t == PACK - 1 and j1 < S:
+                score = keep.tile(
+                    [P, per_bank, width], F32, name="score_last", tag="turn%d" % (c + 1), align_bytes=64
+                )
+            else:
+                score = ring.tile([P, per_bank, width], F32, name="score", bufs=4)
+            nc.vector.tensor_tensor(
+                score[:], bank[:].rearrange("p (s j) -> p s j", s=per_bank),
+                close[:, b0 : b0 + per_bank, t, :], ALU.add,
+            )
+            return score
+
+        def place(c, unit, score):
+            j0, j1 = CHUNKS[c]
+            per_bank = BANK // (j1 - j0)
+            t, b0 = divmod(unit * per_bank, 2)
+            for s in range(per_bank):
+                b = b0 + s
+                nc.vector.tensor_tensor(
+                    pages[b, t][:].indirect(entries(list3, j0, j1)), score[:, s, :], wgo_cols(t, j0, j1), ALU.mult
+                )
+                if j1 == S:
+                    nc.sync.dma_start(sheet_rows(out, b, t), pages[b, t][:])
+
+        staged = {0: first_stage(0)}
+        gather_words(1)
+        waiting = None
+        for c, (j0, j1) in enumerate(CHUNKS):
+            units = 2 * PACK * (j1 - j0) // BANK
+            for unit in range(units):
+                if unit == units - 1 and j1 < S:
+                    staged[c + 1] = first_stage(c + 1)
+                score = add_residual(c, *staged[c], unit)
+                if waiting is not None:
+                    place(*waiting)
+                waiting = (c, unit, score)
+        place(*waiting)

@@ -1,6 +1,8 @@
 from contextlib import ExitStack
+from functools import partial
 
 import concourse.mybir as mybir
+from concourse.masks import make_identity
 
 K, M, H, T, S, T2 = 1024, 512, 1024, 2048, 1024, 2048
 FLOPS = 2 * S * H * (K + M + H)
@@ -19,10 +21,13 @@ ALU = mybir.AluOpType
 P = 128
 PACK = 4
 PASS = P * PACK
+HALF = PASS // 2
 BANK = 512
 LANES = 16
-CHUNKS = ((0, 256), (256, 512), (512, 1024))
-GATHERS = ((0, 512), (512, 1024))
+CHUNKS = ((0, 256), (256, 640), (640, 1024))
+GATHERS = ((0, 640), (640, 1024))
+MIX_ON_VECTOR = ((128, 0),)
+PINS = {(0,5): "before11", (1, 1): "after20", (1, 3): "after21", (1, 5): "before21"}
 
 
 def tile_list_retake_closeness_sheet_kernel(
@@ -33,15 +38,15 @@ def tile_list_retake_closeness_sheet_kernel(
     with ExitStack() as ctx:
         lists = ctx.enter_context(tc.tile_pool(name="lists", bufs=1))
         keep = ctx.enter_context(tc.tile_pool(name="keep", bufs=1))
-        stage = ctx.enter_context(tc.tile_pool(name="stage", bufs=11))
+        stage = ctx.enter_context(tc.tile_pool(name="stage", bufs=8))
         ring = ctx.enter_context(tc.tile_pool(name="ring", bufs=2))
-        psum = ctx.enter_context(tc.psum_pool(name="psum", bufs=4))
+        psum = ctx.enter_context(tc.psum_pool(name="psum", bufs=8))
 
         def big(shape, dtype, name):
             return stage.tile(shape, dtype, name=name, tag="big", align_bytes=64)
 
-        def kept(shape, dtype, name):
-            return keep.tile(shape, dtype, name=name, align_bytes=64)
+        def kept(shape, dtype, name, tag=""):
+            return keep.tile(shape, dtype, name=name, tag=tag, align_bytes=64)
 
         list1 = lists.tile([P, S // LANES], U16, name="list1")
         list2 = lists.tile([P, S // LANES], U16, name="list2")
@@ -52,87 +57,112 @@ def tile_list_retake_closeness_sheet_kernel(
 
         v_bytes = kept([P, T], U8, "v_bytes")
         v2_bytes = kept([P, T], U8, "v2_bytes")
-        w2_bytes = kept([P, H], U8, "w2_bytes")
-        w3_bytes = kept([P, H], U8, "w3_bytes")
-        nc.vector.memset(v_bytes[:].bitcast(I32), 0)
+        w2_plane = kept([P, H], U8, "w2_plane")
+        w3_planes = kept([P, H], U8, "w3_planes")
         nc.gpsimd.memset(v2_bytes[:].bitcast(I32), 0)
-        nc.vector.memset(w2_bytes[:].bitcast(I32), 0)
-        nc.vector.memset(w3_bytes[:].bitcast(I32), 0)
-        for a in range(2):
-            for r in range(2):
-                rows = tab_scales[a].rearrange("(g r) t -> r g t", r=2)[r]
-                nc.scalar.dma_start(v_bytes[:].bitcast(I32)[4 * a + r : P : LANES, :], rows.bitcast(I32))
-        for q in range(4):
-            nc.gpsimd.dma_start(
-                v2_bytes[:].bitcast(I32)[32 * q : 32 * q + 4, :], tab2_scales[0, 4 * q : 4 * q + 4, :].bitcast(I32)
-            )
+        nc.vector.memset(w2_plane[:].bitcast(I32), 0)
+        nc.vector.memset(v_bytes[:].bitcast(I32), 0)
+        nc.vector.memset(w3_planes[:].bitcast(I32), 0)
 
-        def load_table(words, name):
-            table = big([P, T], I32, name)
+        def load_table(table, words):
             nc.sync.dma_start(table[:], words.rearrange("p t i -> p (t i)").bitcast(I32))
             return table
 
-        def load_w1(b, a):
-            raw = big([P, PACK, PASS], F32, "w1_raw%d%d" % (b, a))
-            rows = w1[PASS * a : PASS * (a + 1), PASS * b : PASS * (b + 1)]
+        def load_w1(b, a, raw, c0, c1):
+            rows = w1[PASS * a : PASS * (a + 1), PASS * b + c0 : PASS * b + c1]
             nc.sync.dma_start(raw[:], rows.rearrange("(p i) c -> p i c", i=PACK))
-            return raw
+            w1_raw[b, a, c0] = raw
+
+        def load_plane(plane, scales):
+            passes = scales.shape[0]
+            for q in range(4):
+                nc.gpsimd.dma_start(
+                    plane[:].bitcast(I32)[32 * q : 32 * q + 4 * passes, :],
+                    scales[:, 4 * q : 4 * q + 4, :].bitcast(I32),
+                )
 
         def sheet_rows(sheet, b, t):
             return sheet[PASS * b : PASS * (b + 1), :].rearrange("(p t) c -> p t c", t=PACK)[:, t, :]
 
-        def load_page(b, t):
-            page = big([P, T2], F32, "page%d%d" % (b, t))
-            nc.sync.dma_start(page[:], sheet_rows(page1, b, t))
-            return page
+        factors = {}
 
-        def load_wgo(j0, j1):
-            dealt = kept([P, PACK, j1 - j0], F32, "wgo%d" % j0)
+        def load_wgo(c, tag):
+            j0, j1 = CHUNKS[c]
+            factors[c] = kept([P, PACK, j1 - j0], F32, "wgo%d" % c, tag)
             for q in range(4):
-                nc.sync.dma_start(
-                    dealt[32 * q : 32 * (q + 1), :, :], wgo.rearrange("(i t) j -> i t j", t=PACK)[:, :, j0:j1]
+                nc.gpsimd.dma_start(
+                    factors[c][32 * q : 32 * (q + 1), :, :], wgo.rearrange("(i t) j -> i t j", t=PACK)[:, :, j0:j1]
                 )
-            return dealt
 
-        w1_raw = {}
+        load_plane(v2_bytes, tab2_scales)
+        load_plane(w2_plane, w2_scales)
+        load_plane(w3_planes, w3_scales)
+        ident = kept([P, P], F32, "ident")
+        make_identity(nc, ident[:])
+
+        w1_raw, tables = {}, {}
         nc.sync.dma_start(list1[:], offs)
+        tables[0] = load_table(big([P, T], I32, "table0"), tab_words[0])
+        load_w1(0, 0, big([P, PACK, PASS], F32, "w1_raw00"), 0, PASS)
+        for r in range(2):
+            rows = tab_scales.rearrange("a (g r) t -> r g a t", r=2)[r]
+            nc.sync.dma_start(v_bytes[:].bitcast(I32)[r:P:8, :], rows.bitcast(I32))
+        tables[1] = load_table(big([P, T], I32, "table1"), tab_words[1])
         nc.sync.dma_start(list2[:], offs2)
-        nc.sync.dma_start(list3[:], offs3)
+        load_w1(0, 1, big([P, PACK, PASS], F32, "w1_raw01"), 0, PASS)
+        tables[2] = load_table(kept([P, T], I32, "table2", "late2"), tab2_words[0])
+        w2_codes = kept([P, 2 * H], U8, "w2_codes")
+        nc.sync.dma_start(w2_codes[:].bitcast(I32), w2_words[0].bitcast(I32))
+        load_w1(1, 0, kept([P, PACK, PASS], F32, "w1_raw10", "late0"), 0, PASS)
+        load_w1(1, 1, kept([P, PACK, HALF], F32, "w1_raw11", "late1"), 0, HALF)
+        load_w1(1, 1, big([P, PACK, HALF], F32, "w1_raw_last"), HALF, PASS)
         gains = kept([P, 2, PACK], F32, "gains")
         nc.sync.dma_start(gains[:], gain.rearrange("(b p t) -> p b t", b=2, t=PACK))
-        tables = [load_table(tab_words[0], "table0")]
-        w1_raw[0, 0] = load_w1(0, 0)
-        w2_raw = kept([P, 2 * H], U8, "w2_raw")
-        nc.sync.dma_start(w2_raw[:].bitcast(I32), w2_words[0].bitcast(I32))
-        tables.append(load_table(tab_words[1], "table1"))
-        w1_raw[0, 1] = load_w1(0, 1)
-        tables.append(load_table(tab2_words[0], "table2"))
-        for q in range(4):
-            nc.sync.dma_start(
-                w2_bytes[:].bitcast(I32)[32 * q : 32 * q + 4, :], w2_scales[0, 4 * q : 4 * q + 4, :].bitcast(I32)
-            )
-        w1_raw[1, 0] = load_w1(1, 0)
-        w1_raw[1, 1] = load_w1(1, 1)
-        for q in range(4):
-            nc.sync.dma_start(
-                w3_bytes[:].bitcast(I32)[32 * q : 32 * q + 8, :], w3_scales[:, 4 * q : 4 * q + 4, :].bitcast(I32)
-            )
-        w3_raw = big([P, 2, H], I32, "w3_raw")
-        nc.sync.dma_start(w3_raw[:], w3_words.rearrange("a p c i -> p a (c i)").bitcast(I32))
-        first = CHUNKS[0][1]
-        wgo_first = load_wgo(0, first)
-        order = [(b, t) for t in range(PACK) for b in range(2)]
-        pages = {}
-        for b, t in order[:4]:
-            pages[b, t] = load_page(b, t)
-        wgo_rest = load_wgo(first, S)
-        for b, t in order[4:]:
-            pages[b, t] = load_page(b, t)
+        w3_codes = kept([P, 2, H], I32, "w3_codes")
+        nc.sync.dma_start(w3_codes[:], w3_words.rearrange("a p c i -> p a (c i)").bitcast(I32))
+        nc.sync.dma_start(list3[:], offs3)
 
-        def wgo_cols(t, j0, j1):
-            if j1 <= first:
-                return wgo_first[:, t, j0:j1]
-            return wgo_rest[:, t, j0 - first : j1 - first]
+        order = [(b, t) for b in range(2) for t in range(PACK)]
+        pages = {}
+
+        def load_page(page, b, t):
+            nc.sync.dma_start(page[:], sheet_rows(page1, b, t))
+            pages[b, t] = page
+
+        for n, (b, t) in enumerate(order):
+            load_page(big([P, T2], F32, "page%d%d" % (b, t)), b, t)
+
+        picked = {}
+
+        def gather_words(n, part):
+            j0, j1 = GATHERS[part]
+            words = kept([P, j1 - j0], I32, "picked%d%d" % (n, part), "cast%d" % n if part else "")
+            list_tile = list2 if n == 2 else list1
+            nc.vector.tensor_copy(
+                words[:].bitcast(U32), tables[n][:].bitcast(U32).indirect(entries(list_tile, j0, j1))
+            )
+            picked[n, part] = words
+
+        def picked_cols(n, j):
+            part = 0 if j < GATHERS[0][1] else 1
+            base = GATHERS[part][0]
+            return picked[n, part][:, j - base : j - base + P].bitcast(FP8X4)
+
+        w1_codes, w1_plane = {}, {}
+
+        for b in range(2):
+            for a in range(2):
+                w1_codes[b, a] = kept([P, PASS], U32, "w1_codes%d%d" % (b, a))
+                w1_plane[b, a] = kept([P, PASS], U8, "w1_plane%d%d" % (b, a))
+
+        def quantise_w1(b, a, c0, c1, rounded):
+            dst = rounded[:].rearrange("p (c x i) -> p c i x", i=PACK, x=4)
+            src = w1_raw[b, a, c0][:].rearrange("p i (c x) -> p c i x", x=4)
+            if b == 1:
+                nc.vector.tensor_scalar_mul(dst, src, -1.0)
+            else:
+                nc.scalar.activation(dst, src, ACT.Copy, scale=-1.0)
+            nc.vector.quantize_mx(w1_codes[b, a][:, c0:c1].bitcast(FP8X4), w1_plane[b, a][:, c0:c1], rounded[:])
 
         v_picked = kept([P, S], U8, "v_picked")
         nc.vector.tensor_copy(v_picked[:], v_bytes[:].indirect(list1[:]))
@@ -140,170 +170,213 @@ def tile_list_retake_closeness_sheet_kernel(
         nc.vector.tensor_copy(v_planes[:].bitcast(I32), v_picked[:].bitcast(I32))
         for a in range(2):
             for r in range(2):
-                nc.gpsimd.dma_start(
-                    v_planes[:].bitcast(I32)[4 * a + 2 + r : P : 32, :],
-                    v_picked[:].bitcast(I32)[LANES + 4 * a + r : P : 32, :],
+                nc.scalar.dma_start(
+                    v_planes[:].bitcast(I32)[8 * a + 2 + r : P : 32, :],
+                    v_picked[:].bitcast(I32)[LANES + 8 * a + r : P : 32, :],
                 )
+        gather_words(0, 0)
+        gather_words(1, 0)
         v2_plane = kept([P, S], U8, "v2_plane")
         nc.vector.tensor_copy(v2_plane[:], v2_bytes[:].indirect(list2[:]))
+        gather_words(2, 0)
+        for a in range(2):
+            quantise_w1(0, a, 0, PASS, ring.tile([P, PACK * PASS], BF16, name="w1_rounded", align_bytes=64))
+        quantise_w1(1, 0, 0, PASS, kept([P, PACK * PASS], BF16, "w1_rounded10", "cast0"))
+        quantise_w1(1, 1, 0, HALF, kept([P, PACK * HALF], BF16, "w1_rounded11", "cast1"))
+        quantise_w1(1, 1, HALF, PASS, kept([P, PACK * HALF], BF16, "w1_rounded_last", "cast2"))
 
-        picked = {}
+        load_wgo(0, "late0")
+        load_wgo(1, "late1")
 
-        def gather_words(part):
-            j0, j1 = GATHERS[part]
-            for n, (table, list_tile) in enumerate(zip(tables, (list1, list1, list2))):
-                words = kept([P, j1 - j0], I32, "picked%d%d" % (n, part))
-                nc.vector.tensor_copy(
-                    words[:].bitcast(U32), table[:].bitcast(U32).indirect(entries(list_tile, j0, j1))
-                )
-                picked[n, part] = words
+        close = {}
 
-        def picked_cols(n, j0, j1):
-            part = 0 if j1 <= GATHERS[0][1] else 1
-            base = GATHERS[part][0]
-            return picked[n, part][:, j0 - base : j1 - base].bitcast(FP8X4)
-
-        gather_words(0)
-
-        def deal_bytes(raw, name):
-            dealt = kept([P, H], U8, name)
-            nc.vector.tensor_copy(
-                dealt[:].rearrange("p (b t m) -> p b m t", b=2, t=PACK),
-                raw[:].rearrange("p (b m t) -> p b m t", b=2, t=PACK),
+        def closeness(j, b):
+            bank = psum.tile([P, BANK], F32, name="diff", tag="bank")
+            passes = [
+                (picked_cols(a, j), v_planes[8 * a : P, j : j + P], w1_codes[b, a][:].bitcast(FP8X4), w1_plane[b, a][:])
+                for a in range(2)
+            ]
+            passes.insert(
+                2 if b == 0 else 0,
+                (
+                    picked_cols(2, j), v2_plane[:, j : j + P],
+                    w2_codes[:, 2 * PASS * b : 2 * PASS * (b + 1)].bitcast(FP4X4),
+                    w2_plane[:, PASS * b : PASS * (b + 1)],
+                ),
             )
-            return dealt
-
-        w2_plane = deal_bytes(w2_bytes, "w2_plane")
-        w2_codes = kept([P, 2 * H], U8, "w2_codes")
-        nc.vector.tensor_copy(
-            w2_codes[:].rearrange("p (b t m e) -> p b m t e", b=2, t=PACK, e=2),
-            w2_raw[:].rearrange("p (b m t e) -> p b m t e", b=2, t=PACK, e=2),
-        )
-
-        w1_codes, w1_plane = {}, {}
-        for b in range(2):
-            for a in range(2):
-                rounded = ring.tile([P, PACK * PASS], BF16, name="w1_rounded", align_bytes=64)
-                dst = rounded[:].rearrange("p (t m i) -> p m t i", t=PACK, i=PACK)
-                src = w1_raw[b, a][:].rearrange("p i (m t) -> p m t i", t=PACK)
-                if (b, a) == (1, 1):
-                    nc.vector.tensor_scalar_mul(dst, src, -1.0)
-                else:
-                    nc.scalar.activation(dst, src, ACT.Copy, scale=-1.0)
-                w1_codes[b, a] = kept([P, PASS], U32, "w1_codes%d%d" % (b, a))
-                w1_plane[b, a] = kept([P, PASS], U8, "w1_plane%d%d" % (b, a))
-                nc.vector.quantize_mx(w1_codes[b, a][:].bitcast(FP8X4), w1_plane[b, a][:], rounded[:])
-
-        w3_planes = deal_bytes(w3_bytes, "w3_planes")
-        w3_codes = kept([P, 2 * H], I32, "w3_codes")
-        nc.vector.tensor_copy(
-            w3_codes[:].bitcast(U32).rearrange("p (h t m) -> p h m t", t=PACK, m=P),
-            w3_raw[:].bitcast(U32).rearrange("p a (b m t) -> p (a b) m t", t=PACK, m=P),
-        )
-
-        def first_stage(c):
-            j0, j1 = CHUNKS[c]
-            width = j1 - j0
-            per_bank = BANK // width
-            close = kept([P, 2, PACK, width], F32, "close%d" % c)
-            z_ops = []
-            for b in range(2):
-                for t0 in range(0, PACK, per_bank):
-                    bank = psum.tile([P, BANK], F32, name="diff")
-                    for s in range(per_bank):
-                        t = t0 + s
-                        acc = bank[:, s * width : (s + 1) * width]
-                        col = PASS * b + P * t
-                        nc.tensor.matmul_mx(
-                            acc, lhsT=w2_codes[:, 2 * col : 2 * (col + P)].bitcast(FP4X4),
-                            lhsT_scale=w2_plane[:, col : col + P],
-                            rhs=picked_cols(2, j0, j1), rhs_scale=v2_plane[:, j0:j1], start=True, stop=False,
-                        )
-                        for a in range(2):
-                            nc.tensor.matmul_mx(
-                                acc, lhsT=w1_codes[b, a][:, P * t : P * (t + 1)].bitcast(FP8X4),
-                                lhsT_scale=w1_plane[b, a][:, P * t : P * (t + 1)],
-                                rhs=picked_cols(a, j0, j1), rhs_scale=v_planes[4 * a : P, j0:j1],
-                                start=False, stop=(a == 1),
-                            )
-                    part = close[:, b, t0 : t0 + per_bank, :].rearrange("p t j -> p (t j)")
-                    nc.scalar.activation(part, bank[:], ACT.Abs)
-                    nc.scalar.activation(part, part, ACT.Exp, scale=-1.0)
-                if c > 0 and b == 1:
-                    woven = keep.tile([P, PACK * width], BF16, name="woven_last", tag="turn%d" % c, align_bytes=64)
-                else:
-                    woven = ring.tile([P, PACK * width], BF16, name="woven", align_bytes=64)
-                walk_out = woven[:].rearrange("p (c i t) -> p c t i", t=PACK, i=4)
-                if c == 0:
-                    nc.vector.tensor_tensor(
-                        walk_out,
-                        close[:, b].rearrange("p t (c i) -> p c t i", i=4),
-                        gains[:, b, :].unsqueeze(1).unsqueeze(3).to_broadcast([P, width // 4, PACK, 4]),
-                        ALU.mult,
-                    )
-                else:
-                    scaled = ring.tile([P, PACK, width], BF16, name="scaled", align_bytes=64)
-                    for t in range(PACK):
-                        nc.scalar.activation(
-                            scaled[:, t, :], close[:, b, t, :], ACT.Copy, scale=gains[:, b, t : t + 1]
-                        )
-                    nc.scalar.copy(walk_out, scaled[:].rearrange("p t (c i) -> p c t i", i=4))
-                z_codes = kept([P, width], U32, "z_codes%d%d" % (c, b))
-                z_plane = kept([P, width], U8, "z_plane%d%d" % (c, b))
-                nc.vector.quantize_mx(z_codes[:].bitcast(FP8X4), z_plane[:], woven[:])
-                z_ops.append((z_codes, z_plane))
-            return close, z_ops
-
-        def add_residual(c, close, z_ops, unit):
-            j0, j1 = CHUNKS[c]
-            width = j1 - j0
-            per_bank = BANK // width
-            t, b0 = divmod(unit * per_bank, 2)
-            bank = psum.tile([P, BANK], F32, name="mixed")
-            for s in range(per_bank):
-                col = PASS * (b0 + s) + P * t
-                for a in range(2):
-                    nc.tensor.matmul_mx(
-                        bank[:, s * width : (s + 1) * width],
-                        lhsT=w3_codes[:, H * a + col : H * a + col + P].bitcast(FP8X4),
-                        lhsT_scale=w3_planes[4 * a : P, col : col + P],
-                        rhs=z_ops[a][0][:].bitcast(FP8X4), rhs_scale=z_ops[a][1][:],
-                        start=(a == 0), stop=(a == 1),
-                    )
-            if t == PACK - 1 and j1 < S:
-                score = keep.tile(
-                    [P, per_bank, width], F32, name="score_last", tag="turn%d" % (c + 1), align_bytes=64
+            for n, (lhsT, lhsT_scale, rhs, rhs_scale) in enumerate(passes):
+                nc.tensor.matmul_mx(
+                    bank[:], lhsT=lhsT, lhsT_scale=lhsT_scale, rhs=rhs, rhs_scale=rhs_scale,
+                    start=(n == 0), stop=(n == 2),
                 )
-            else:
-                score = ring.tile([P, per_bank, width], F32, name="score", bufs=4)
+            near = kept([P, PACK, P], F32, "close%d_%d" % (j, b))
+            nc.scalar.activation(near[:], bank[:].rearrange("p (m t) -> p t m", t=PACK), ACT.Abs)
+            nc.scalar.activation(near[:], near[:], ACT.Exp, scale=-1.0)
+            close[j, b] = near
+
+        z_ops, wovens = {}, {}
+
+        def blocks(c):
+            return range(CHUNKS[c][0], CHUNKS[c][1], P)
+
+        def weave_on_vector(woven, j, at, b):
+            bank = psum.tile([P, PACK, P], F32, name="turned", tag="bank")
+            for t in range(PACK):
+                nc.tensor.transpose(bank[:, t, :], close[j, b][:, t, :], ident[:])
             nc.vector.tensor_tensor(
-                score[:], bank[:].rearrange("p (s j) -> p s j", s=per_bank),
-                close[:, b0 : b0 + per_bank, t, :], ALU.add,
+                woven[:, PACK * at : PACK * (at + P)].rearrange("p (x t) -> p x t", t=PACK),
+                bank[:].rearrange("p t x -> p x t"),
+                gains[:, b, :].unsqueeze(1).to_broadcast([P, P, PACK]),
+                ALU.mult,
             )
-            return score
 
-        def place(c, unit, score):
+        def scale_on_scalar(scaled, j0, j1, b, t):
+            bank = psum.tile([P, j1 - j0], F32, name="turned", tag="bank")
+            for j in range(j0, j1, P):
+                nc.tensor.transpose(bank[:, j - j0 : j - j0 + P], close[j, b][:, t, :], ident[:])
+            nc.scalar.activation(scaled[:, t, :], bank[:], ACT.Copy, scale=gains[:, b, t : t + 1])
+
+        def weave_on_scalar(woven, scaled):
+            nc.scalar.copy(
+                woven[:].rearrange("p (c x t) -> p c t x", t=PACK, x=4),
+                scaled[:].rearrange("p t (c x) -> p c t x", x=4),
+            )
+
+        def quantise_z(j0, j1, b, woven, tag=""):
+            z_codes = kept([P, j1 - j0], U32, "z_codes%d_%d" % (j0, b), tag)
+            z_plane = kept([P, j1 - j0], U8, "z_plane%d_%d" % (j0, b))
+            nc.vector.quantize_mx(z_codes[:].bitcast(FP8X4), z_plane[:], woven[:])
+            for j in range(j0, j1, P):
+                z_ops[j, b] = (z_codes[:, j - j0 : j - j0 + P], z_plane[:, j - j0 : j - j0 + P])
+
+        def z_on_vector(j0, j1, b):
+            woven = ring.tile([P, PACK * (j1 - j0)], BF16, name="woven", align_bytes=64)
+            for j in range(j0, j1, P):
+                weave_on_vector(woven, j, j - j0, b)
+            quantise_z(j0, j1, b, woven)
+
+        def z_on_scalar(c, b):
             j0, j1 = CHUNKS[c]
-            per_bank = BANK // (j1 - j0)
-            t, b0 = divmod(unit * per_bank, 2)
-            for s in range(per_bank):
-                b = b0 + s
-                nc.vector.tensor_tensor(
-                    pages[b, t][:].indirect(entries(list3, j0, j1)), score[:, s, :], wgo_cols(t, j0, j1), ALU.mult
-                )
-                if j1 == S:
-                    nc.sync.dma_start(sheet_rows(out, b, t), pages[b, t][:])
+            scaled = ring.tile([P, PACK, j1 - j0], BF16, name="scaled", align_bytes=64)
+            for t in range(PACK):
+                scale_on_scalar(scaled, j0, j1, b, t)
+            woven = kept([P, PACK * (j1 - j0)], BF16, "woven%d%d" % (c, b), "before%d%d" % (c, b))
+            weave_on_scalar(woven, scaled)
+            wovens[c, b] = woven
 
-        staged = {0: first_stage(0)}
-        gather_words(1)
-        waiting = None
-        for c, (j0, j1) in enumerate(CHUNKS):
-            units = 2 * PACK * (j1 - j0) // BANK
-            for unit in range(units):
-                if unit == units - 1 and j1 < S:
-                    staged[c + 1] = first_stage(c + 1)
-                score = add_residual(c, *staged[c], unit)
-                if waiting is not None:
-                    place(*waiting)
-                waiting = (c, unit, score)
-        place(*waiting)
+        def quantise_chunk(c, b):
+            quantise_z(*CHUNKS[c], b, wovens[c, b], "after%d%d" % (c, b))
+
+        def weave_chunk(c, b, j):
+            j0, j1 = CHUNKS[c]
+            if j == j0:
+                wovens[c, b] = kept([P, PACK * (j1 - j0)], BF16, "woven%d%d" % (c, b), "before%d%d" % (c, b))
+            weave_on_vector(wovens[c, b], j, j - j0, b)
+
+        mixed = {}
+
+        def mix(j, b):
+            bank = psum.tile([P, BANK], F32, name="product", tag="bank")
+            for a in range(2):
+                nc.tensor.matmul_mx(
+                    bank[:], lhsT=z_ops[j, a][0].bitcast(FP8X4), lhsT_scale=z_ops[j, a][1],
+                    rhs=w3_codes[:, a, PASS * b : PASS * (b + 1)].bitcast(FP8X4),
+                    rhs_scale=w3_planes[4 * a : P, PASS * b : PASS * (b + 1)],
+                    start=(a == 0), stop=(a == 1),
+                )
+            mixed[j, b] = ring.tile([P, PACK, P], F32, name="mixed", bufs=6)
+            if (j, b) in MIX_ON_VECTOR:
+                nc.vector.tensor_copy(mixed[j, b][:], bank[:].rearrange("p (m t) -> p t m", t=PACK))
+            else:
+                nc.scalar.copy(mixed[j, b][:], bank[:].rearrange("p (m t) -> p t m", t=PACK))
+
+        def place(c, n):
+            j0, j1 = CHUNKS[c]
+            b, t = order[n]
+            bank = psum.tile([P, j1 - j0], F32, name="summed", tag="bank")
+            for j in blocks(c):
+                cols = bank[:, j - j0 : j - j0 + P]
+                nc.tensor.matmul(cols, close[j, b][:, t, :], ident[:], start=True, stop=False, is_transpose=True)
+                nc.tensor.matmul(cols, mixed[j, b][:, t, :], ident[:], start=False, stop=True, is_transpose=True)
+            if (c, n) in PINS:
+                score = kept([P, j1 - j0], F32, "score%d%d" % (c, n), PINS[c, n])
+            else:
+                score = ring.tile([P, j1 - j0], F32, name="score", bufs=10)
+            nc.scalar.copy(score[:], bank[:])
+            nc.vector.tensor_tensor(
+                pages[b, t][:].indirect(entries(list3, j0, j1)), score[:], factors[c][:, t, :], ALU.mult
+            )
+            if j1 == S:
+                nc.sync.dma_start(sheet_rows(out, b, t), pages[b, t][:])
+
+        closeness(0, 0)
+        closeness(128, 0)
+        closeness(256, 0)
+        closeness(0, 1)
+        closeness(128, 1)
+        closeness(384, 0)
+        z_on_vector(0, 256, 0)
+        closeness(512, 0)
+        z_on_scalar(1, 0)
+        quantise_chunk(1, 0)
+        z_on_vector(0, 128, 1)
+        z_on_vector(128, 256, 1)
+        gather_words(0, 1)
+        gather_words(1, 1)
+        gather_words(2, 1)
+        load_wgo(2, "late2")
+        mix(0, 0)
+        mix(128, 0)
+        place(0, 0)
+        mix(0, 1)
+        mix(128, 1)
+        closeness(256, 1)
+        place(0, 1)
+        closeness(384, 1)
+        place(0, 2)
+        closeness(512, 1)
+        place(0, 3)
+        closeness(640, 0)
+        place(0, 4)
+        z_on_scalar(1, 1)
+        quantise_chunk(1, 1)
+        place(0, 5)
+        place(0, 6)
+        closeness(768, 0)
+        place(0, 7)
+        mix(256, 0)
+        mix(384, 0)
+        mix(512, 0)
+        closeness(896, 0)
+        place(1, 0)
+        mix(256, 1)
+        mix(384, 1)
+        mix(512, 1)
+        place(1, 1)
+        z_on_scalar(2, 0)
+        quantise_chunk(2, 0)
+        closeness(640, 1)
+        place(1, 2)
+        closeness(768, 1)
+        closeness(896, 1)
+        place(1, 3)
+        place(1, 4)
+        z_on_scalar(2, 1)
+        quantise_chunk(2, 1)
+        place(1, 5)
+        mix(640, 0)
+        mix(768, 0)
+        mix(896, 0)
+        place(1, 6)
+        place(1, 7)
+        place(2, 0)
+        mix(640, 1)
+        mix(768, 1)
+        mix(896, 1)
+        place(2, 1)
+        place(2, 2)
+        place(2, 3)
+        place(2, 4)
+        place(2, 5)
+        place(2, 6)
+        place(2, 7)

from contextlib import ExitStack
from functools import partial

import concourse.mybir as mybir
from concourse.masks import make_identity

K, M, H, T, S, T2 = 1024, 512, 1024, 2048, 1024, 2048
FLOPS = 2 * S * H * (K + M + H)

F32 = mybir.dt.float32
BF16 = mybir.dt.bfloat16
I32 = mybir.dt.int32
U32 = mybir.dt.uint32
U16 = mybir.dt.uint16
U8 = mybir.dt.uint8
FP8X4 = mybir.dt.float8_e4m3fn_x4
FP4X4 = mybir.dt.float4_e2m1fn_x4
ACT = mybir.ActivationFunctionType
ALU = mybir.AluOpType

P = 128
PACK = 4
PASS = P * PACK
HALF = PASS // 2
BANK = 512
LANES = 16
CHUNKS = ((0, 256), (256, 640), (640, 1024))
GATHERS = ((0, 640), (640, 1024))
MIX_ON_VECTOR = ((128, 0),)
PINS = {(0,5): "before11", (1, 1): "after20", (1, 3): "after21", (1, 5): "before21"}


def tile_list_retake_closeness_sheet_kernel(
    tc, tab_words, tab_scales, tab2_words, tab2_scales, offs, offs2, offs3, w1,
    w2_words, w2_scales, w3_words, w3_scales, gain, page1, wgo, out,
):
    nc = tc.nc
    with ExitStack() as ctx:
        lists = ctx.enter_context(tc.tile_pool(name="lists", bufs=1))
        keep = ctx.enter_context(tc.tile_pool(name="keep", bufs=1))
        stage = ctx.enter_context(tc.tile_pool(name="stage", bufs=8))
        ring = ctx.enter_context(tc.tile_pool(name="ring", bufs=2))
        psum = ctx.enter_context(tc.psum_pool(name="psum", bufs=8))

        def big(shape, dtype, name):
            return stage.tile(shape, dtype, name=name, tag="big", align_bytes=64)

        def kept(shape, dtype, name, tag=""):
            return keep.tile(shape, dtype, name=name, tag=tag, align_bytes=64)

        list1 = lists.tile([P, S // LANES], U16, name="list1")
        list2 = lists.tile([P, S // LANES], U16, name="list2")
        list3 = lists.tile([P, S // LANES], U16, name="list3")

        def entries(list_tile, j0, j1):
            return list_tile[:, j0 // LANES : j1 // LANES]

        v_bytes = kept([P, T], U8, "v_bytes")
        v2_bytes = kept([P, T], U8, "v2_bytes")
        w2_plane = kept([P, H], U8, "w2_plane")
        w3_planes = kept([P, H], U8, "w3_planes")
        nc.gpsimd.memset(v2_bytes[:].bitcast(I32), 0)
        nc.vector.memset(w2_plane[:].bitcast(I32), 0)
        nc.vector.memset(v_bytes[:].bitcast(I32), 0)
        nc.vector.memset(w3_planes[:].bitcast(I32), 0)

        def load_table(table, words):
            nc.sync.dma_start(table[:], words.rearrange("p t i -> p (t i)").bitcast(I32))
            return table

        def load_w1(b, a, raw, c0, c1):
            rows = w1[PASS * a : PASS * (a + 1), PASS * b + c0 : PASS * b + c1]
            nc.sync.dma_start(raw[:], rows.rearrange("(p i) c -> p i c", i=PACK))
            w1_raw[b, a, c0] = raw

        def load_plane(plane, scales):
            passes = scales.shape[0]
            for q in range(4):
                nc.gpsimd.dma_start(
                    plane[:].bitcast(I32)[32 * q : 32 * q + 4 * passes, :],
                    scales[:, 4 * q : 4 * q + 4, :].bitcast(I32),
                )

        def sheet_rows(sheet, b, t):
            return sheet[PASS * b : PASS * (b + 1), :].rearrange("(p t) c -> p t c", t=PACK)[:, t, :]

        factors = {}

        def load_wgo(c, tag):
            j0, j1 = CHUNKS[c]
            factors[c] = kept([P, PACK, j1 - j0], F32, "wgo%d" % c, tag)
            for q in range(4):
                nc.gpsimd.dma_start(
                    factors[c][32 * q : 32 * (q + 1), :, :], wgo.rearrange("(i t) j -> i t j", t=PACK)[:, :, j0:j1]
                )

        load_plane(v2_bytes, tab2_scales)
        load_plane(w2_plane, w2_scales)
        load_plane(w3_planes, w3_scales)
        ident = kept([P, P], F32, "ident")
        make_identity(nc, ident[:])

        w1_raw, tables = {}, {}
        nc.sync.dma_start(list1[:], offs)
        tables[0] = load_table(big([P, T], I32, "table0"), tab_words[0])
        load_w1(0, 0, big([P, PACK, PASS], F32, "w1_raw00"), 0, PASS)
        for r in range(2):
            rows = tab_scales.rearrange("a (g r) t -> r g a t", r=2)[r]
            nc.sync.dma_start(v_bytes[:].bitcast(I32)[r:P:8, :], rows.bitcast(I32))
        tables[1] = load_table(big([P, T], I32, "table1"), tab_words[1])
        nc.sync.dma_start(list2[:], offs2)
        load_w1(0, 1, big([P, PACK, PASS], F32, "w1_raw01"), 0, PASS)
        tables[2] = load_table(kept([P, T], I32, "table2", "late2"), tab2_words[0])
        w2_codes = kept([P, 2 * H], U8, "w2_codes")
        nc.sync.dma_start(w2_codes[:].bitcast(I32), w2_words[0].bitcast(I32))
        load_w1(1, 0, kept([P, PACK, PASS], F32, "w1_raw10", "late0"), 0, PASS)
        load_w1(1, 1, kept([P, PACK, HALF], F32, "w1_raw11", "late1"), 0, HALF)
        load_w1(1, 1, big([P, PACK, HALF], F32, "w1_raw_last"), HALF, PASS)
        gains = kept([P, 2, PACK], F32, "gains")
        nc.sync.dma_start(gains[:], gain.rearrange("(b p t) -> p b t", b=2, t=PACK))
        w3_codes = kept([P, 2, H], I32, "w3_codes")
        nc.sync.dma_start(w3_codes[:], w3_words.rearrange("a p c i -> p a (c i)").bitcast(I32))
        nc.sync.dma_start(list3[:], offs3)

        order = [(b, t) for b in range(2) for t in range(PACK)]
        pages = {}

        def load_page(page, b, t):
            nc.sync.dma_start(page[:], sheet_rows(page1, b, t))
            pages[b, t] = page

        for n, (b, t) in enumerate(order):
            load_page(big([P, T2], F32, "page%d%d" % (b, t)), b, t)

        picked = {}

        def gather_words(n, part):
            j0, j1 = GATHERS[part]
            words = kept([P, j1 - j0], I32, "picked%d%d" % (n, part), "cast%d" % n if part else "")
            list_tile = list2 if n == 2 else list1
            nc.vector.tensor_copy(
                words[:].bitcast(U32), tables[n][:].bitcast(U32).indirect(entries(list_tile, j0, j1))
            )
            picked[n, part] = words

        def picked_cols(n, j):
            part = 0 if j < GATHERS[0][1] else 1
            base = GATHERS[part][0]
            return picked[n, part][:, j - base : j - base + P].bitcast(FP8X4)

        w1_codes, w1_plane = {}, {}

        for b in range(2):
            for a in range(2):
                w1_codes[b, a] = kept([P, PASS], U32, "w1_codes%d%d" % (b, a))
                w1_plane[b, a] = kept([P, PASS], U8, "w1_plane%d%d" % (b, a))

        def quantise_w1(b, a, c0, c1, rounded):
            dst = rounded[:].rearrange("p (c x i) -> p c i x", i=PACK, x=4)
            src = w1_raw[b, a, c0][:].rearrange("p i (c x) -> p c i x", x=4)
            if b == 1:
                nc.vector.tensor_scalar_mul(dst, src, -1.0)
            else:
                nc.scalar.activation(dst, src, ACT.Copy, scale=-1.0)
            nc.vector.quantize_mx(w1_codes[b, a][:, c0:c1].bitcast(FP8X4), w1_plane[b, a][:, c0:c1], rounded[:])

        v_picked = kept([P, S], U8, "v_picked")
        nc.vector.tensor_copy(v_picked[:], v_bytes[:].indirect(list1[:]))
        v_planes = kept([P, S], U8, "v_planes")
        nc.vector.tensor_copy(v_planes[:].bitcast(I32), v_picked[:].bitcast(I32))
        for a in range(2):
            for r in range(2):
                nc.scalar.dma_start(
                    v_planes[:].bitcast(I32)[8 * a + 2 + r : P : 32, :],
                    v_picked[:].bitcast(I32)[LANES + 8 * a + r : P : 32, :],
                )
        gather_words(0, 0)
        gather_words(1, 0)
        v2_plane = kept([P, S], U8, "v2_plane")
        nc.vector.tensor_copy(v2_plane[:], v2_bytes[:].indirect(list2[:]))
        gather_words(2, 0)
        for a in range(2):
            quantise_w1(0, a, 0, PASS, ring.tile([P, PACK * PASS], BF16, name="w1_rounded", align_bytes=64))
        quantise_w1(1, 0, 0, PASS, kept([P, PACK * PASS], BF16, "w1_rounded10", "cast0"))
        quantise_w1(1, 1, 0, HALF, kept([P, PACK * HALF], BF16, "w1_rounded11", "cast1"))
        quantise_w1(1, 1, HALF, PASS, kept([P, PACK * HALF], BF16, "w1_rounded_last", "cast2"))

        load_wgo(0, "late0")
        load_wgo(1, "late1")

        close = {}

        def closeness(j, b):
            bank = psum.tile([P, BANK], F32, name="diff", tag="bank")
            passes = [
                (picked_cols(a, j), v_planes[8 * a : P, j : j + P], w1_codes[b, a][:].bitcast(FP8X4), w1_plane[b, a][:])
                for a in range(2)
            ]
            passes.insert(
                2 if b == 0 else 0,
                (
                    picked_cols(2, j), v2_plane[:, j : j + P],
                    w2_codes[:, 2 * PASS * b : 2 * PASS * (b + 1)].bitcast(FP4X4),
                    w2_plane[:, PASS * b : PASS * (b + 1)],
                ),
            )
            for n, (lhsT, lhsT_scale, rhs, rhs_scale) in enumerate(passes):
                nc.tensor.matmul_mx(
                    bank[:], lhsT=lhsT, lhsT_scale=lhsT_scale, rhs=rhs, rhs_scale=rhs_scale,
                    start=(n == 0), stop=(n == 2),
                )
            near = kept([P, PACK, P], F32, "close%d_%d" % (j, b))
            nc.scalar.activation(near[:], bank[:].rearrange("p (m t) -> p t m", t=PACK), ACT.Abs)
            nc.scalar.activation(near[:], near[:], ACT.Exp, scale=-1.0)
            close[j, b] = near

        z_ops, wovens = {}, {}

        def blocks(c):
            return range(CHUNKS[c][0], CHUNKS[c][1], P)

        def weave_on_vector(woven, j, at, b):
            bank = psum.tile([P, PACK, P], F32, name="turned", tag="bank")
            for t in range(PACK):
                nc.tensor.transpose(bank[:, t, :], close[j, b][:, t, :], ident[:])
            nc.vector.tensor_tensor(
                woven[:, PACK * at : PACK * (at + P)].rearrange("p (x t) -> p x t", t=PACK),
                bank[:].rearrange("p t x -> p x t"),
                gains[:, b, :].unsqueeze(1).to_broadcast([P, P, PACK]),
                ALU.mult,
            )

        def scale_on_scalar(scaled, j0, j1, b, t):
            bank = psum.tile([P, j1 - j0], F32, name="turned", tag="bank")
            for j in range(j0, j1, P):
                nc.tensor.transpose(bank[:, j - j0 : j - j0 + P], close[j, b][:, t, :], ident[:])
            nc.scalar.activation(scaled[:, t, :], bank[:], ACT.Copy, scale=gains[:, b, t : t + 1])

        def weave_on_scalar(woven, scaled):
            nc.scalar.copy(
                woven[:].rearrange("p (c x t) -> p c t x", t=PACK, x=4),
                scaled[:].rearrange("p t (c x) -> p c t x", x=4),
            )

        def quantise_z(j0, j1, b, woven, tag=""):
            z_codes = kept([P, j1 - j0], U32, "z_codes%d_%d" % (j0, b), tag)
            z_plane = kept([P, j1 - j0], U8, "z_plane%d_%d" % (j0, b))
            nc.vector.quantize_mx(z_codes[:].bitcast(FP8X4), z_plane[:], woven[:])
            for j in range(j0, j1, P):
                z_ops[j, b] = (z_codes[:, j - j0 : j - j0 + P], z_plane[:, j - j0 : j - j0 + P])

        def z_on_vector(j0, j1, b):
            woven = ring.tile([P, PACK * (j1 - j0)], BF16, name="woven", align_bytes=64)
            for j in range(j0, j1, P):
                weave_on_vector(woven, j, j - j0, b)
            quantise_z(j0, j1, b, woven)

        def z_on_scalar(c, b):
            j0, j1 = CHUNKS[c]
            scaled = ring.tile([P, PACK, j1 - j0], BF16, name="scaled", align_bytes=64)
            for t in range(PACK):
                scale_on_scalar(scaled, j0, j1, b, t)
            woven = kept([P, PACK * (j1 - j0)], BF16, "woven%d%d" % (c, b), "before%d%d" % (c, b))
            weave_on_scalar(woven, scaled)
            wovens[c, b] = woven

        def quantise_chunk(c, b):
            quantise_z(*CHUNKS[c], b, wovens[c, b], "after%d%d" % (c, b))

        def weave_chunk(c, b, j):
            j0, j1 = CHUNKS[c]
            if j == j0:
                wovens[c, b] = kept([P, PACK * (j1 - j0)], BF16, "woven%d%d" % (c, b), "before%d%d" % (c, b))
            weave_on_vector(wovens[c, b], j, j - j0, b)

        mixed = {}

        def mix(j, b):
            bank = psum.tile([P, BANK], F32, name="product", tag="bank")
            for a in range(2):
                nc.tensor.matmul_mx(
                    bank[:], lhsT=z_ops[j, a][0].bitcast(FP8X4), lhsT_scale=z_ops[j, a][1],
                    rhs=w3_codes[:, a, PASS * b : PASS * (b + 1)].bitcast(FP8X4),
                    rhs_scale=w3_planes[4 * a : P, PASS * b : PASS * (b + 1)],
                    start=(a == 0), stop=(a == 1),
                )
            mixed[j, b] = ring.tile([P, PACK, P], F32, name="mixed", bufs=6)
            if (j, b) in MIX_ON_VECTOR:
                nc.vector.tensor_copy(mixed[j, b][:], bank[:].rearrange("p (m t) -> p t m", t=PACK))
            else:
                nc.scalar.copy(mixed[j, b][:], bank[:].rearrange("p (m t) -> p t m", t=PACK))

        def place(c, n):
            j0, j1 = CHUNKS[c]
            b, t = order[n]
            bank = psum.tile([P, j1 - j0], F32, name="summed", tag="bank")
            for j in blocks(c):
                cols = bank[:, j - j0 : j - j0 + P]
                nc.tensor.matmul(cols, close[j, b][:, t, :], ident[:], start=True, stop=False, is_transpose=True)
                nc.tensor.matmul(cols, mixed[j, b][:, t, :], ident[:], start=False, stop=True, is_transpose=True)
            if (c, n) in PINS:
                score = kept([P, j1 - j0], F32, "score%d%d" % (c, n), PINS[c, n])
            else:
                score = ring.tile([P, j1 - j0], F32, name="score", bufs=10)
            nc.scalar.copy(score[:], bank[:])
            nc.vector.tensor_tensor(
                pages[b, t][:].indirect(entries(list3, j0, j1)), score[:], factors[c][:, t, :], ALU.mult
            )
            if j1 == S:
                nc.sync.dma_start(sheet_rows(out, b, t), pages[b, t][:])

        closeness(0, 0)
        closeness(128, 0)
        closeness(256, 0)
        closeness(0, 1)
        closeness(128, 1)
        closeness(384, 0)
        z_on_vector(0, 256, 0)
        closeness(512, 0)
        z_on_scalar(1, 0)
        quantise_chunk(1, 0)
        z_on_vector(0, 128, 1)
        z_on_vector(128, 256, 1)
        gather_words(0, 1)
        gather_words(1, 1)
        gather_words(2, 1)
        load_wgo(2, "late2")
        mix(0, 0)
        mix(128, 0)
        place(0, 0)
        mix(0, 1)
        mix(128, 1)
        closeness(256, 1)
        place(0, 1)
        closeness(384, 1)
        place(0, 2)
        closeness(512, 1)
        place(0, 3)
        closeness(640, 0)
        place(0, 4)
        z_on_scalar(1, 1)
        quantise_chunk(1, 1)
        place(0, 5)
        place(0, 6)
        closeness(768, 0)
        place(0, 7)
        mix(256, 0)
        mix(384, 0)
        mix(512, 0)
        closeness(896, 0)
        place(1, 0)
        mix(256, 1)
        mix(384, 1)
        mix(512, 1)
        place(1, 1)
        z_on_scalar(2, 0)
        quantise_chunk(2, 0)
        closeness(640, 1)
        place(1, 2)
        closeness(768, 1)
        closeness(896, 1)
        place(1, 3)
        place(1, 4)
        z_on_scalar(2, 1)
        quantise_chunk(2, 1)
        place(1, 5)
        mix(640, 0)
        mix(768, 0)
        mix(896, 0)
        place(1, 6)
        place(1, 7)
        place(2, 0)
        mix(640, 1)
        mix(768, 1)
        mix(896, 1)
        place(2, 1)
        place(2, 2)
        place(2, 3)
        place(2, 4)
        place(2, 5)
        place(2, 6)
        place(2, 7)
